import numpy as np
import ml_dtypes


def mxq(x, axis, fmt="e4m3"):
    dtype, down = {"e4m3": (ml_dtypes.float8_e4m3fn, 7), "e5m2": (ml_dtypes.float8_e5m2, 14)}[fmt]
    v = np.moveaxis(np.asarray(x, np.float32).astype(ml_dtypes.bfloat16).astype(np.float64), axis, -1)
    blocks = v.reshape(v.shape[:-1] + (-1, 32))
    amax = np.abs(blocks).max(-1, keepdims=True)
    byte = np.maximum(np.where(amax > 0, np.frexp(amax)[1] - 1 + 127, 0) - down, 1)
    scale = np.exp2(byte - 127.0)
    codes = (blocks / scale).astype(np.float32).astype(dtype).astype(np.float64)
    return np.moveaxis((codes * scale).reshape(v.shape), -1, axis)


WIDE = False


def mx_kscale(k):
    if not WIDE:
        return np.ones(k)
    levels = np.array([10, -10, 5, -5, 0])
    if k % 512:
        return np.exp2(np.random.permutation(np.resize(levels, k // 32))).repeat(32)
    a = np.empty((k // 512, 16))
    for p in range(k // 512):
        a[p, :8] = np.random.permutation(np.resize(levels, 8))
        for g in range(8):
            far = levels[np.abs(levels - a[p, g]) >= 10]
            a[p, g + 8] = far[np.random.randint(len(far))]
    return np.exp2(a.ravel()).repeat(32)


def f64(x):
    return np.asarray(x).astype(np.float64)


def striped(idx):
    return np.tile(idx.reshape(-1, 16).T, (8, 1)).astype(np.uint16)


def unstriped(offs):
    return offs[:16].T.reshape(-1).astype(np.int64)


E2M1 = np.array([0.0, 0.5, 1.0, 1.5, 2.0, 3.0, 4.0, 6.0, -0.0, -0.5, -1.0, -1.5, -2.0, -3.0, -4.0, -6.0])


def pack_weight(w, fmt):
    k, n = w.shape
    w = f64(np.asarray(w, np.float32).astype(ml_dtypes.bfloat16)).reshape(k // 32, 32, n)
    amax = np.abs(w).max(1)
    if fmt == "e4m3":
        byte = np.frexp(amax)[1] - 1 + 127 - 7
    else:
        mant, ex = np.frexp(amax / 6.0)
        byte = np.where(mant > 0.5, ex, ex - 1) + 127
    byte = np.clip(np.where(amax > 0, byte, 1), 1, 254)
    scaled = (w * np.exp2(127.0 - byte)[:, None, :]).reshape(k, n).astype(np.float32)
    by_word = np.ascontiguousarray(scaled.reshape(k // 512, 128, 4, n).transpose(0, 1, 3, 2))
    if fmt == "e4m3":
        words = by_word.astype(ml_dtypes.float8_e4m3fn).view(np.uint8)
    else:
        c = by_word.astype(ml_dtypes.float4_e2m1fn).view(np.uint8) & 0xF
        words = (c[..., 0::2] | (c[..., 1::2] << 4)).reshape(k // 512, 128, 2 * n)
    return np.ascontiguousarray(words), np.ascontiguousarray(byte.astype(np.uint8).reshape(k // 512, 16, n))


def unpack_weight(words, scales, fmt):
    g, _, n = scales.shape
    words = np.ascontiguousarray(words).reshape(g, 128, n, -1)
    if fmt == "e4m3":
        vals = words.view(ml_dtypes.float8_e4m3fn).astype(np.float64)
    else:
        nib = np.empty((g, 128, n, 4), np.uint8)
        nib[..., 0::2] = words & 0xF
        nib[..., 1::2] = words >> 4
        vals = E2M1[nib]
    vals = vals * np.repeat(np.exp2(scales.astype(np.float64) - 127.0), 8, axis=1)[..., None]
    return vals.transpose(0, 1, 3, 2).reshape(g * 512, n)


def gelu(v):
    return 0.5 * v * (1.0 + np.tanh(np.sqrt(2.0 / np.pi) * (v + 0.044715 * v**3)))


def bf(x):
    return np.asarray(x, np.float32).astype(ml_dtypes.bfloat16)


def planes(Y):
    n, m = Y.shape
    b = f64(bf(Y)).reshape(n // 32, 32, m)
    amax = np.abs(b).max(1)
    byte = np.clip(np.where(amax > 0, np.frexp(amax)[1] - 1 + 127 - 7, 1), 1, 254)
    codes = (b * np.exp2(127.0 - byte)[:, None, :]).reshape(n, m).astype(np.float32).astype(ml_dtypes.float8_e4m3fn).view(np.uint8)
    words = codes.reshape(n // 512, 128, 4, m).transpose(0, 1, 3, 2)
    return np.ascontiguousarray(words), np.ascontiguousarray(byte.astype(np.uint8).reshape(n // 512, 16, m))


K, H, N, T, S, T2, P = 512, 1024, 768, 2048, 1024, 2048, 1024

def setup_inputs():
    n = np.random.standard_normal
    s = mx_kscale(K)[:, None]
    u = mx_kscale(H)[:, None]
    d = {}
    d["tab_words"], d["tab_scales"] = pack_weight(n((K, T)) * s, "e4m3")
    d["offs"] = striped(np.random.permutation(T)[:S])
    d["wa"] = (n((K, H)) / s / K ** 0.5).astype(np.float32)
    d["wb_words"], d["wb_scales"] = pack_weight(n((K, H)) / s / K ** 0.5, "e4m3")
    d["gain"] = (np.exp(0.3 * n(H)) * u[:, 0]).astype(np.float32)
    d["wgs"] = np.exp(0.3 * n((128, S))).astype(np.float32)
    d["offs2"] = striped(np.random.permutation(T2)[:S])
    d["page0"] = (n((H, T2)) * u).astype(np.float32)
    d["offs3"] = striped(np.random.permutation(T2)[:P])
    d["bias"] = (0.7 * n(H) * u[:, 0]).astype(np.float32)
    d["w2_words"], d["w2_scales"] = pack_weight(n((H, N)) / u / H ** 0.5, "e2m1")
    d["chart"] = np.exp(0.4 * n((N, P))).astype(np.float32)
    return d

def reference(tab_words, tab_scales, offs, wa, wb_words, wb_scales, gain, wgs, offs2, page0,
              offs3, bias, w2_words, w2_scales, chart):
    v = unpack_weight(tab_words, tab_scales, "e4m3")[:, unstriped(offs)]
    a = mxq(f64(wa), 0, "e4m3").T @ v
    b = unpack_weight(wb_words, wb_scales, "e4m3").T @ v
    h = f64(gain)[:, None] * np.abs(a - b)
    page = f64(page0).copy()
    page[:, unstriped(offs2)] = np.tile(f64(wgs), (H // 128, 1)) * h
    x = page[:, unstriped(offs3)] + f64(bias)[:, None]
    g = unpack_weight(w2_words, w2_scales, "e2m1").T @ mxq(x, 0, "e4m3")
    y = f64(chart) * np.tanh(g)
    words, scales = planes(page)
    return y, page, words, scales

@@ -1,0 +1,320 @@
+from contextlib import ExitStack
+
+import concourse.mybir as mybir
+
+K, H, N, T, S, T2, M = 512, 1024, 768, 2048, 1024, 2048, 1024
+FLOPS = 2 * (2 * K * H * S + H * N * M)
+
+F32 = mybir.dt.float32
+BF16 = mybir.dt.bfloat16
+I32 = mybir.dt.int32
+U32 = mybir.dt.uint32
+U16 = mybir.dt.uint16
+U8 = mybir.dt.uint8
+E4M3 = mybir.dt.float8_e4m3fn_x4
+E2M1 = mybir.dt.float4_e2m1fn_x4
+ACT = mybir.ActivationFunctionType
+MULT = mybir.AluOpType.mult
+
+P = 128
+PACK = 4
+GROUPS = H // (P * PACK)
+SLICES = GROUPS * PACK
+BANK = 512
+LIST_COLS = BANK // 16
+QUADS = 4
+
+
+def tile_list_crane_sway_page_kernel(
+    tc, tab_words, tab_scales, offs, wa, wb_words, wb_scales, gain, wgs, offs2, page0,
+    offs3, bias, w2_words, w2_scales, chart, out_0, out_1, out_2, out_3,
+):
+    nc = tc.nc
+    with ExitStack() as ctx:
+        lists = ctx.enter_context(tc.tile_pool(name="lists", bufs=1))
+        keep = ctx.enter_context(tc.tile_pool(name="keep", bufs=1))
+        ring = ctx.enter_context(tc.tile_pool(name="ring", bufs=1))
+        ps1 = ctx.enter_context(tc.psum_pool(name="ps1", bufs=1))
+        ps2 = ctx.enter_context(tc.psum_pool(name="ps2", bufs=6))
+
+        def big(shape, dtype, name):
+            return ring.tile(shape, dtype, name=name, tag="big", bufs=3, align_bytes=64)
+
+        def half(i):
+            return slice(i * BANK, (i + 1) * BANK)
+
+        def list_half(i):
+            return slice(i * LIST_COLS, (i + 1) * LIST_COLS)
+
+        def load_scale_rows(queue, plane, rows):
+            for q in range(QUADS):
+                queue.dma_start(plane[32 * q : 32 * q + 4], rows[4 * q : 4 * q + 4])
+
+        def fill_scale_rows(plane, rows):
+            for q in range(QUADS):
+                four = rows[4 * q : 4 * q + 4]
+                nc.sync.dma_start(plane[32 * q : 32 * q + 32], four.unsqueeze(0).to_broadcast([8, 4, four.shape[1]]))
+
+        idx1 = lists.tile([P, S // 16], U16, name="idx1")
+        idx2 = lists.tile([P, S // 16], U16, name="idx2")
+        idx3 = lists.tile([P, M // 16], U16, name="idx3")
+        tab_w = big([P, T], U32, "tab_w")
+        tab_s = keep.tile([P, T], U8, name="tab_s", align_bytes=64)
+        wb_s_raw = keep.tile([P, H], U8, name="wb_s_raw", align_bytes=64)
+        w2_s = keep.tile([P, GROUPS, N], U8, name="w2_s", align_bytes=64)
+        nc.gpsimd.memset(wb_s_raw[:].bitcast(I32), 0)
+
+        nc.sync.dma_start(idx1[:], offs)
+        fill_scale_rows(tab_s[:].bitcast(I32), tab_scales[0].bitcast(I32))
+        nc.sync.dma_start(tab_w[:].bitcast(I32), tab_words[0].rearrange("p c i -> p (c i)").bitcast(I32))
+        gain_sb = keep.tile([P, GROUPS, PACK], F32, name="gain_sb")
+        bias_sb = keep.tile([P, GROUPS, PACK], F32, name="bias_sb")
+        nc.gpsimd.memset(w2_s[:].bitcast(I32), 0)
+
+        wa_rows = wa.rearrange("(p j) c -> p j c", j=PACK)
+        wb_rows = wb_words[0].rearrange("p c i -> p (c i)").bitcast(I32)
+        wgs_rows = wgs.rearrange("(q t) j -> q t j", t=PACK)
+        page_rows = page0.rearrange("(g p t) c -> g t p c", p=P, t=PACK)
+        out1_rows = out_1.rearrange("(g p t) c -> g t p c", p=P, t=PACK)
+
+        wa_raw, wb_raw, pages = [], [], []
+
+        def load_weights(g):
+            wa_raw.append(big([P, PACK, BANK], F32, "wa_raw%d" % g))
+            nc.sync.dma_start(wa_raw[g][:], wa_rows[:, :, half(g)])
+            wb_raw.append(keep.tile([P, BANK], I32, name="wb_raw%d" % g))
+            nc.sync.dma_start(wb_raw[g][:], wb_rows[:, half(g)])
+
+        def load_page(i):
+            pages.append(keep.tile([P, T2], F32, name="page%d" % i))
+            nc.sync.dma_start(pages[i][:], page_rows[i // PACK, i % PACK])
+
+        def load_factors(t0, t1):
+            factors = keep.tile([P, t1 - t0, S], F32, name="wgs%d" % t0)
+            for q in range(QUADS):
+                nc.sync.dma_start(factors[32 * q : 32 * q + 32], wgs_rows[:, t0:t1, :])
+            return [factors[:, t, :] for t in range(t1 - t0)]
+
+        load_weights(0)
+        nc.sync.dma_start(gain_sb[:], gain.rearrange("(g p t) -> p g t", p=P, t=PACK))
+        load_scale_rows(nc.sync, wb_s_raw[:].bitcast(I32), wb_scales[0].bitcast(I32))
+        load_page(0)
+        nc.sync.dma_start(idx2[:], offs2)
+        wgs_sb = load_factors(0, 1)
+        wgs_sb = wgs_sb + load_factors(1, 2)
+        load_page(1)
+        nc.sync.dma_start(idx3[:], offs3)
+        nc.sync.dma_start(bias_sb[:], bias.rearrange("(g p t) -> p g t", p=P, t=PACK))
+        load_weights(1)
+        wgs_sb = wgs_sb + load_factors(2, PACK)
+        for i in range(2, SLICES):
+            load_page(i)
+        w2_w = keep.tile([P, GROUPS, 2 * N], U8, name="w2_w", align_bytes=64)
+        nc.sync.dma_start(w2_w[:].bitcast(I32), w2_words.bitcast(I32).rearrange("g p c -> p g c"))
+        load_scale_rows(nc.sync, w2_s[:].bitcast(I32), w2_scales.bitcast(I32).rearrange("g q c -> q g c"))
+
+        v_w, v_s = [], []
+        for hf in range(S // BANK):
+            v_s.append(keep.tile([P, BANK], U8, name="v_s%d" % hf, align_bytes=64))
+            v_w.append(keep.tile([P, BANK], U32, name="v_w%d" % hf, align_bytes=64))
+
+        def look_up(hf):
+            nc.vector.tensor_copy(v_s[hf][:], tab_s[:].indirect(idx1[:, list_half(hf)]))
+            nc.vector.tensor_copy(v_w[hf][:], tab_w[:].indirect(idx1[:, list_half(hf)]))
+
+        wa_w = keep.tile([P, H], U32, name="wa_w", align_bytes=64)
+        wa_s = keep.tile([P, H], U8, name="wa_s", align_bytes=64)
+        wb_w = keep.tile([P, H], I32, name="wb_w", align_bytes=64)
+        wb_s = keep.tile([P, H], U8, name="wb_s", align_bytes=64)
+
+        def woven_tile(name):
+            return ring.tile([P, PACK * BANK], BF16, name=name, tag="woven", bufs=3, align_bytes=64)
+
+        def deal_wb_words(g):
+            nc.vector.tensor_copy(
+                wb_w[:, half(g)].rearrange("p (t m) -> p t m", t=PACK),
+                wb_raw[g][:].rearrange("p (m t) -> p t m", t=PACK),
+            )
+
+        def deal_wb_scales(g):
+            nc.vector.tensor_copy(
+                wb_s[:, half(g)].rearrange("p (t m) -> p t m", t=PACK),
+                wb_s_raw[:, half(g)].rearrange("p (m t) -> p t m", t=PACK),
+            )
+
+        def round_wa(g, dealt, t0, t1):
+            nc.scalar.activation(
+                dealt[:].rearrange("p (t m j) -> p m t j", t=PACK, j=PACK)[:, :, t0:t1, :],
+                wa_raw[g][:].rearrange("p j (m t) -> p m t j", t=PACK)[:, :, t0:t1, :],
+                ACT.Copy, scale=-1.0,
+            )
+
+        def quantise_wa(g, dealt, t0, t1):
+            cols = slice(g * BANK + t0 * P, g * BANK + t1 * P)
+            nc.vector.quantize_mx(wa_w[:, cols].bitcast(E4M3), wa_s[:, cols], dealt[:, t0 * BANK : t1 * BANK])
+
+        sizes = {}
+
+        def first_stage(i, halves):
+            if i not in sizes:
+                sizes[i] = ring.tile([P, S], F32, name="size%d" % i, tag="size", bufs=3)
+            cols = slice(i * P, (i + 1) * P)
+            for hf in halves:
+                acc = ps1.tile([P, BANK], F32, name="acc1", tag="acc1_%d" % hf)
+                nc.tensor.matmul_mx(acc[:], wa_w[:, cols].bitcast(E4M3), wa_s[:, cols],
+                                    v_w[hf][:].bitcast(E4M3), v_s[hf][:], start=True, stop=False)
+                nc.tensor.matmul_mx(acc[:], wb_w[:, cols].bitcast(E4M3), wb_s[:, cols],
+                                    v_w[hf][:].bitcast(E4M3), v_s[hf][:], start=False, stop=True)
+                nc.scalar.activation(sizes[i][:, half(hf)], acc[:], ACT.Abs)
+
+        def apply_gain(i, halves):
+            span = slice(halves[0] * BANK, (halves[-1] + 1) * BANK)
+            nc.scalar.activation(sizes[i][:, span], sizes[i][:, span], ACT.Copy,
+                                 scale=gain_sb[:, i // PACK, i % PACK : i % PACK + 1])
+
+        def put(i, halves):
+            factors = wgs_sb[i % PACK]
+            span = slice(halves[0] * BANK, (halves[-1] + 1) * BANK)
+            cols = slice(halves[0] * LIST_COLS, (halves[-1] + 1) * LIST_COLS)
+            nc.vector.tensor_tensor(pages[i][:].indirect(idx2[:, cols]), sizes[i][:, span], factors[:, span], MULT)
+
+        picked = {}
+
+        def fetch(i, halves):
+            if i not in picked:
+                tag = "picked_spare" if i == SLICES - 2 else "picked"
+                picked[i] = ring.tile([P, M], F32, name="picked%d" % i, tag=tag, bufs=1)
+            span = slice(halves[0] * BANK, (halves[-1] + 1) * BANK)
+            cols = slice(halves[0] * LIST_COLS, (halves[-1] + 1) * LIST_COLS)
+            nc.vector.tensor_copy(picked[i][:, span], pages[i][:].indirect(idx3[:, cols]))
+
+        page_pairs = [keep.tile([P, 2, T2, 2], BF16, name="page_pairs%d" % g) for g in range(GROUPS)]
+        x_pairs = [keep.tile([P, 2, M, 2], BF16, name="x_pairs%d" % g) for g in range(GROUPS)]
+
+        def round_page(i, cols):
+            t = i % PACK
+            nc.scalar.copy(page_pairs[i // PACK][:, t // 2, cols, t % 2], pages[i][:, cols])
+
+        def round_x(i, cols):
+            t = i % PACK
+            nc.scalar.activation(x_pairs[i // PACK][:, t // 2, cols, t % 2], picked[i][:, cols], ACT.Identity,
+                                 bias=bias_sb[:, i // PACK, t : t + 1])
+
+        def weave(move, pairs, c):
+            woven = woven_tile("woven")
+            words = pairs[:].rearrange("p u m e -> p u (m e)").bitcast(F32)
+            move(woven[:].bitcast(F32).rearrange("p (m u) -> p m u", u=2),
+                 words[:, :, half(c)].rearrange("p u m -> p m u"))
+            return woven
+
+        plane_s = [keep.tile([P, T2], U8, name="plane_s%d" % g, align_bytes=64) for g in range(GROUPS)]
+
+        def quantise_page(g, c, woven):
+            plane_w = ring.tile([P, BANK], U32, name="plane_w", tag="plane_w", bufs=4, align_bytes=64)
+            nc.vector.quantize_mx(plane_w[:].bitcast(E4M3), plane_s[g][:, half(c)], woven[:])
+            nc.sync.dma_start(out_2[g].rearrange("p m t -> p (m t)").bitcast(I32)[:, half(c)], plane_w[:].bitcast(I32))
+
+        def store_plane_scales(g):
+            for q in range(QUADS):
+                nc.sync.dma_start(out_3[g].bitcast(I32)[4 * q : 4 * q + 4], plane_s[g][:].bitcast(I32)[32 * q : 32 * q + 4])
+
+        x_w, x_s = {}, {}
+
+        def quantise_x(g, c, woven):
+            x_w[g, c] = keep.tile([P, BANK], U32, name="x_w%d%d" % (g, c), align_bytes=64)
+            x_s[g, c] = keep.tile([P, BANK], U8, name="x_s%d%d" % (g, c), align_bytes=64)
+            nc.vector.quantize_mx(x_w[g, c][:].bitcast(E4M3), x_s[g, c][:], woven[:])
+
+        charts = []
+
+        def score(n, c):
+            acc = ps2.tile([P, BANK], F32, name="acc2")
+            for g in range(GROUPS):
+                nc.tensor.matmul_mx(acc[:], w2_w[:, g, 2 * n * P : 2 * (n + 1) * P].bitcast(E2M1),
+                                    w2_s[:, g, n * P : (n + 1) * P], x_w[g, c][:].bitcast(E4M3), x_s[g, c][:],
+                                    start=(g == 0), stop=(g == GROUPS - 1))
+            bent = ring.tile([P, BANK], F32, name="bent", tag="size", bufs=3)
+            nc.scalar.activation(bent[:], acc[:], ACT.Tanh)
+            return bent
+
+        def finish(n, c, bent):
+            factor = charts[n // 2][:, n % 2, half(c)]
+            nc.vector.tensor_tensor(factor, bent[:], factor, MULT)
+            nc.sync.dma_start(out_0[n * P : (n + 1) * P, half(c)], factor)
+
+        look_up(0)
+        dealt0 = woven_tile("dealt0")
+        round_wa(0, dealt0, 0, 1)
+        quantise_wa(0, dealt0, 0, 1)
+        deal_wb_words(0)
+        deal_wb_scales(0)
+        first_stage(0, [0])
+        nc.vector.tensor_scalar(sizes[0][:, half(0)], sizes[0][:, half(0)], gain_sb[:, 0, 0:1], None, MULT)
+        look_up(1)
+        first_stage(0, [1])
+        apply_gain(0, [1])
+        round_wa(0, dealt0, 1, 2)
+        round_wa(0, dealt0, 2, 4)
+        quantise_wa(0, dealt0, 1, 2)
+        quantise_wa(0, dealt0, 2, 4)
+        deal_wb_scales(1)
+        put(0, [0])
+        put(0, [1])
+        first_stage(1, [0, 1])
+        apply_gain(1, [0, 1])
+        dealt1 = woven_tile("dealt1")
+        round_wa(1, dealt1, 0, PACK)
+        deal_wb_words(1)
+        quantise_wa(1, dealt1, 0, PACK)
+        chart_rows = chart.rearrange("(j s p) m -> j p s m", s=2, p=P)
+        for j in range(N // (2 * P)):
+            charts.append(big([P, 2, M], F32, "chart%d" % j))
+            nc.sync.dma_start(charts[j][:], chart_rows[j])
+
+        later = {4: [("page", 0), ("page", 1)], 5: [("x", 0), ("x", 1)], 6: [("page", 2), ("page", 3)]}
+        last = SLICES - 1
+        for i in range(last):
+            if i + 2 < SLICES:
+                first_stage(i + 2, [0, 1])
+            for kind, c in later.get(i, []):
+                if kind == "x":
+                    quantise_x(0, c, weave(nc.scalar.copy, x_pairs[0], c))
+                else:
+                    quantise_page(0, c, weave(nc.scalar.copy, page_pairs[0], c))
+            if i > 0:
+                put(i, [0, 1])
+                fetch(i - 1, [0, 1])
+            nc.sync.dma_start(out1_rows[i // PACK, i % PACK], pages[i][:])
+            round_page(i, slice(0, T2))
+            if i > 0:
+                round_x(i - 1, slice(0, M))
+            if i + 2 < SLICES:
+                apply_gain(i + 2, [0, 1])
+        store_plane_scales(0)
+
+        fetch(last - 1, [0, 1])
+        round_x(last - 1, slice(0, M))
+        put(last, [0, 1])
+        nc.sync.dma_start(out1_rows[last // PACK, last % PACK], pages[last][:])
+        fetch(last, [0])
+        fetch(last, [1])
+        round_page(last, half(0))
+        round_page(last, half(1))
+        wp0 = weave(nc.scalar.copy, page_pairs[1], 0)
+        round_x(last, half(0))
+        round_x(last, half(1))
+        quantise_page(1, 0, wp0)
+        wx0 = weave(nc.vector.tensor_copy, x_pairs[1], 0)
+        wx1 = weave(nc.vector.tensor_copy, x_pairs[1], 1)
+        quantise_x(1, 0, wx0)
+        quantise_x(1, 1, wx1)
+        round_page(last, half(2))
+        round_page(last, half(3))
+        quantise_page(1, 1, weave(nc.scalar.copy, page_pairs[1], 1))
+        units = [(n, c) for c in range(M // BANK) for n in range(N // P)]
+        for u, (n, c) in enumerate(units):
+            finish(n, c, score(n, c))
+            if u in (2, 5):
+                quantise_page(1, 2 + u // 3, weave(nc.scalar.copy, page_pairs[1], 2 + u // 3))
+            if u == 5:
+                store_plane_scales(1)

@@ -23,6 +23,7 @@ SLICES = GROUPS * PACK
 BANK = 512
 LIST_COLS = BANK // 16
 QUADS = 4
+RUN = 4
 
 
 def tile_list_crane_sway_page_kernel(
@@ -188,23 +189,22 @@ def tile_list_crane_sway_page_kernel(
             cols = slice(halves[0] * LIST_COLS, (halves[-1] + 1) * LIST_COLS)
             nc.vector.tensor_copy(picked[i][:, span], pages[i][:].indirect(idx3[:, cols]))
 
-        page_pairs = [keep.tile([P, 2, T2, 2], BF16, name="page_pairs%d" % g) for g in range(GROUPS)]
-        x_pairs = [keep.tile([P, 2, M, 2], BF16, name="x_pairs%d" % g) for g in range(GROUPS)]
+        page_pairs = [keep.tile([P, PACK, T2], BF16, name="page_pairs%d" % g) for g in range(GROUPS)]
+        x_pairs = [keep.tile([P, PACK, M], BF16, name="x_pairs%d" % g) for g in range(GROUPS)]
 
         def round_page(i, cols):
             t = i % PACK
-            nc.scalar.copy(page_pairs[i // PACK][:, t // 2, cols, t % 2], pages[i][:, cols])
+            nc.scalar.copy(page_pairs[i // PACK][:, t, cols], pages[i][:, cols])
 
         def round_x(i, cols):
             t = i % PACK
-            nc.scalar.activation(x_pairs[i // PACK][:, t // 2, cols, t % 2], picked[i][:, cols], ACT.Identity,
+            nc.scalar.activation(x_pairs[i // PACK][:, t, cols], picked[i][:, cols], ACT.Identity,
                                  bias=bias_sb[:, i // PACK, t : t + 1])
 
         def weave(move, pairs, c):
             woven = woven_tile("woven")
-            words = pairs[:].rearrange("p u m e -> p u (m e)").bitcast(F32)
-            move(woven[:].bitcast(F32).rearrange("p (m u) -> p m u", u=2),
-                 words[:, :, half(c)].rearrange("p u m -> p m u"))
+            move(woven[:].rearrange("p (c i t) -> p c t i", i=RUN, t=PACK),
+                 pairs[:, :, half(c)].rearrange("p t (c i) -> p c t i", i=RUN))
             return woven
 
         plane_s = [keep.tile([P, T2], U8, name="plane_s%d" % g, align_bytes=64) for g in range(GROUPS)]
@@ -313,8 +313,12 @@ def tile_list_crane_sway_page_kernel(
         quantise_page(1, 1, weave(nc.scalar.copy, page_pairs[1], 1))
         units = [(n, c) for c in range(M // BANK) for n in range(N // P)]
         for u, (n, c) in enumerate(units):
-            finish(n, c, score(n, c))
-            if u in (2, 5):
-                quantise_page(1, 2 + u // 3, weave(nc.scalar.copy, page_pairs[1], 2 + u // 3))
-            if u == 5:
+            if u == 0:
+                wp3 = weave(nc.vector.tensor_copy, page_pairs[1], 3)
+            bent = score(n, c)
+            finish(n, c, bent)
+            if u == 0:
+                quantise_page(1, 3, wp3)
+            if u == 3:
+                quantise_page(1, 2, weave(nc.scalar.copy, page_pairs[1], 2))
                 store_plane_scales(1)

from contextlib import ExitStack

import concourse.mybir as mybir

K, H, N, T, S, T2, M = 512, 1024, 768, 2048, 1024, 2048, 1024
FLOPS = 2 * (2 * K * H * S + H * N * M)

F32 = mybir.dt.float32
BF16 = mybir.dt.bfloat16
I32 = mybir.dt.int32
U32 = mybir.dt.uint32
U16 = mybir.dt.uint16
U8 = mybir.dt.uint8
E4M3 = mybir.dt.float8_e4m3fn_x4
E2M1 = mybir.dt.float4_e2m1fn_x4
ACT = mybir.ActivationFunctionType
MULT = mybir.AluOpType.mult

P = 128
PACK = 4
GROUPS = H // (P * PACK)
SLICES = GROUPS * PACK
BANK = 512
LIST_COLS = BANK // 16
QUADS = 4
RUN = 4


def tile_list_crane_sway_page_kernel(
    tc, tab_words, tab_scales, offs, wa, wb_words, wb_scales, gain, wgs, offs2, page0,
    offs3, bias, w2_words, w2_scales, chart, out_0, out_1, out_2, out_3,
):
    nc = tc.nc
    with ExitStack() as ctx:
        lists = ctx.enter_context(tc.tile_pool(name="lists", bufs=1))
        keep = ctx.enter_context(tc.tile_pool(name="keep", bufs=1))
        ring = ctx.enter_context(tc.tile_pool(name="ring", bufs=1))
        ps1 = ctx.enter_context(tc.psum_pool(name="ps1", bufs=1))
        ps2 = ctx.enter_context(tc.psum_pool(name="ps2", bufs=6))

        def big(shape, dtype, name):
            return ring.tile(shape, dtype, name=name, tag="big", bufs=3, align_bytes=64)

        def half(i):
            return slice(i * BANK, (i + 1) * BANK)

        def list_half(i):
            return slice(i * LIST_COLS, (i + 1) * LIST_COLS)

        def load_scale_rows(queue, plane, rows):
            for q in range(QUADS):
                queue.dma_start(plane[32 * q : 32 * q + 4], rows[4 * q : 4 * q + 4])

        def fill_scale_rows(plane, rows):
            for q in range(QUADS):
                four = rows[4 * q : 4 * q + 4]
                nc.sync.dma_start(plane[32 * q : 32 * q + 32], four.unsqueeze(0).to_broadcast([8, 4, four.shape[1]]))

        idx1 = lists.tile([P, S // 16], U16, name="idx1")
        idx2 = lists.tile([P, S // 16], U16, name="idx2")
        idx3 = lists.tile([P, M // 16], U16, name="idx3")
        tab_w = big([P, T], U32, "tab_w")
        tab_s = keep.tile([P, T], U8, name="tab_s", align_bytes=64)
        wb_s_raw = keep.tile([P, H], U8, name="wb_s_raw", align_bytes=64)
        w2_s = keep.tile([P, GROUPS, N], U8, name="w2_s", align_bytes=64)
        nc.gpsimd.memset(wb_s_raw[:].bitcast(I32), 0)

        nc.sync.dma_start(idx1[:], offs)
        fill_scale_rows(tab_s[:].bitcast(I32), tab_scales[0].bitcast(I32))
        nc.sync.dma_start(tab_w[:].bitcast(I32), tab_words[0].rearrange("p c i -> p (c i)").bitcast(I32))
        gain_sb = keep.tile([P, GROUPS, PACK], F32, name="gain_sb")
        bias_sb = keep.tile([P, GROUPS, PACK], F32, name="bias_sb")
        nc.gpsimd.memset(w2_s[:].bitcast(I32), 0)

        wa_rows = wa.rearrange("(p j) c -> p j c", j=PACK)
        wb_rows = wb_words[0].rearrange("p c i -> p (c i)").bitcast(I32)
        wgs_rows = wgs.rearrange("(q t) j -> q t j", t=PACK)
        page_rows = page0.rearrange("(g p t) c -> g t p c", p=P, t=PACK)
        out1_rows = out_1.rearrange("(g p t) c -> g t p c", p=P, t=PACK)

        wa_raw, wb_raw, pages = [], [], []

        def load_weights(g):
            wa_raw.append(big([P, PACK, BANK], F32, "wa_raw%d" % g))
            nc.sync.dma_start(wa_raw[g][:], wa_rows[:, :, half(g)])
            wb_raw.append(keep.tile([P, BANK], I32, name="wb_raw%d" % g))
            nc.sync.dma_start(wb_raw[g][:], wb_rows[:, half(g)])

        def load_page(i):
            pages.append(keep.tile([P, T2], F32, name="page%d" % i))
            nc.sync.dma_start(pages[i][:], page_rows[i // PACK, i % PACK])

        def load_factors(t0, t1):
            factors = keep.tile([P, t1 - t0, S], F32, name="wgs%d" % t0)
            for q in range(QUADS):
                nc.sync.dma_start(factors[32 * q : 32 * q + 32], wgs_rows[:, t0:t1, :])
            return [factors[:, t, :] for t in range(t1 - t0)]

        load_weights(0)
        nc.sync.dma_start(gain_sb[:], gain.rearrange("(g p t) -> p g t", p=P, t=PACK))
        load_scale_rows(nc.sync, wb_s_raw[:].bitcast(I32), wb_scales[0].bitcast(I32))
        load_page(0)
        nc.sync.dma_start(idx2[:], offs2)
        wgs_sb = load_factors(0, 1)
        wgs_sb = wgs_sb + load_factors(1, 2)
        load_page(1)
        nc.sync.dma_start(idx3[:], offs3)
        nc.sync.dma_start(bias_sb[:], bias.rearrange("(g p t) -> p g t", p=P, t=PACK))
        load_weights(1)
        wgs_sb = wgs_sb + load_factors(2, PACK)
        for i in range(2, SLICES):
            load_page(i)
        w2_w = keep.tile([P, GROUPS, 2 * N], U8, name="w2_w", align_bytes=64)
        nc.sync.dma_start(w2_w[:].bitcast(I32), w2_words.bitcast(I32).rearrange("g p c -> p g c"))
        load_scale_rows(nc.sync, w2_s[:].bitcast(I32), w2_scales.bitcast(I32).rearrange("g q c -> q g c"))

        v_w, v_s = [], []
        for hf in range(S // BANK):
            v_s.append(keep.tile([P, BANK], U8, name="v_s%d" % hf, align_bytes=64))
            v_w.append(keep.tile([P, BANK], U32, name="v_w%d" % hf, align_bytes=64))

        def look_up(hf):
            nc.vector.tensor_copy(v_s[hf][:], tab_s[:].indirect(idx1[:, list_half(hf)]))
            nc.vector.tensor_copy(v_w[hf][:], tab_w[:].indirect(idx1[:, list_half(hf)]))

        wa_w = keep.tile([P, H], U32, name="wa_w", align_bytes=64)
        wa_s = keep.tile([P, H], U8, name="wa_s", align_bytes=64)
        wb_w = keep.tile([P, H], I32, name="wb_w", align_bytes=64)
        wb_s = keep.tile([P, H], U8, name="wb_s", align_bytes=64)

        def woven_tile(name):
            return ring.tile([P, PACK * BANK], BF16, name=name, tag="woven", bufs=3, align_bytes=64)

        def deal_wb_words(g):
            nc.vector.tensor_copy(
                wb_w[:, half(g)].rearrange("p (t m) -> p t m", t=PACK),
                wb_raw[g][:].rearrange("p (m t) -> p t m", t=PACK),
            )

        def deal_wb_scales(g):
            nc.vector.tensor_copy(
                wb_s[:, half(g)].rearrange("p (t m) -> p t m", t=PACK),
                wb_s_raw[:, half(g)].rearrange("p (m t) -> p t m", t=PACK),
            )

        def round_wa(g, dealt, t0, t1):
            nc.scalar.activation(
                dealt[:].rearrange("p (t m j) -> p m t j", t=PACK, j=PACK)[:, :, t0:t1, :],
                wa_raw[g][:].rearrange("p j (m t) -> p m t j", t=PACK)[:, :, t0:t1, :],
                ACT.Copy, scale=-1.0,
            )

        def quantise_wa(g, dealt, t0, t1):
            cols = slice(g * BANK + t0 * P, g * BANK + t1 * P)
            nc.vector.quantize_mx(wa_w[:, cols].bitcast(E4M3), wa_s[:, cols], dealt[:, t0 * BANK : t1 * BANK])

        sizes = {}

        def first_stage(i, halves):
            if i not in sizes:
                sizes[i] = ring.tile([P, S], F32, name="size%d" % i, tag="size", bufs=3)
            cols = slice(i * P, (i + 1) * P)
            for hf in halves:
                acc = ps1.tile([P, BANK], F32, name="acc1", tag="acc1_%d" % hf)
                nc.tensor.matmul_mx(acc[:], wa_w[:, cols].bitcast(E4M3), wa_s[:, cols],
                                    v_w[hf][:].bitcast(E4M3), v_s[hf][:], start=True, stop=False)
                nc.tensor.matmul_mx(acc[:], wb_w[:, cols].bitcast(E4M3), wb_s[:, cols],
                                    v_w[hf][:].bitcast(E4M3), v_s[hf][:], start=False, stop=True)
                nc.scalar.activation(sizes[i][:, half(hf)], acc[:], ACT.Abs)

        def apply_gain(i, halves):
            span = slice(halves[0] * BANK, (halves[-1] + 1) * BANK)
            nc.scalar.activation(sizes[i][:, span], sizes[i][:, span], ACT.Copy,
                                 scale=gain_sb[:, i // PACK, i % PACK : i % PACK + 1])

        def put(i, halves):
            factors = wgs_sb[i % PACK]
            span = slice(halves[0] * BANK, (halves[-1] + 1) * BANK)
            cols = slice(halves[0] * LIST_COLS, (halves[-1] + 1) * LIST_COLS)
            nc.vector.tensor_tensor(pages[i][:].indirect(idx2[:, cols]), sizes[i][:, span], factors[:, span], MULT)

        picked = {}

        def fetch(i, halves):
            if i not in picked:
                tag = "picked_spare" if i == SLICES - 2 else "picked"
                picked[i] = ring.tile([P, M], F32, name="picked%d" % i, tag=tag, bufs=1)
            span = slice(halves[0] * BANK, (halves[-1] + 1) * BANK)
            cols = slice(halves[0] * LIST_COLS, (halves[-1] + 1) * LIST_COLS)
            nc.vector.tensor_copy(picked[i][:, span], pages[i][:].indirect(idx3[:, cols]))

        page_pairs = [keep.tile([P, PACK, T2], BF16, name="page_pairs%d" % g) for g in range(GROUPS)]
        x_pairs = [keep.tile([P, PACK, M], BF16, name="x_pairs%d" % g) for g in range(GROUPS)]

        def round_page(i, cols):
            t = i % PACK
            nc.scalar.copy(page_pairs[i // PACK][:, t, cols], pages[i][:, cols])

        def round_x(i, cols):
            t = i % PACK
            nc.scalar.activation(x_pairs[i // PACK][:, t, cols], picked[i][:, cols], ACT.Identity,
                                 bias=bias_sb[:, i // PACK, t : t + 1])

        def weave(move, pairs, c):
            woven = woven_tile("woven")
            move(woven[:].rearrange("p (c i t) -> p c t i", i=RUN, t=PACK),
                 pairs[:, :, half(c)].rearrange("p t (c i) -> p c t i", i=RUN))
            return woven

        plane_s = [keep.tile([P, T2], U8, name="plane_s%d" % g, align_bytes=64) for g in range(GROUPS)]

        def quantise_page(g, c, woven):
            plane_w = ring.tile([P, BANK], U32, name="plane_w", tag="plane_w", bufs=4, align_bytes=64)
            nc.vector.quantize_mx(plane_w[:].bitcast(E4M3), plane_s[g][:, half(c)], woven[:])
            nc.sync.dma_start(out_2[g].rearrange("p m t -> p (m t)").bitcast(I32)[:, half(c)], plane_w[:].bitcast(I32))

        def store_plane_scales(g):
            for q in range(QUADS):
                nc.sync.dma_start(out_3[g].bitcast(I32)[4 * q : 4 * q + 4], plane_s[g][:].bitcast(I32)[32 * q : 32 * q + 4])

        x_w, x_s = {}, {}

        def quantise_x(g, c, woven):
            x_w[g, c] = keep.tile([P, BANK], U32, name="x_w%d%d" % (g, c), align_bytes=64)
            x_s[g, c] = keep.tile([P, BANK], U8, name="x_s%d%d" % (g, c), align_bytes=64)
            nc.vector.quantize_mx(x_w[g, c][:].bitcast(E4M3), x_s[g, c][:], woven[:])

        charts = []

        def score(n, c):
            acc = ps2.tile([P, BANK], F32, name="acc2")
            for g in range(GROUPS):
                nc.tensor.matmul_mx(acc[:], w2_w[:, g, 2 * n * P : 2 * (n + 1) * P].bitcast(E2M1),
                                    w2_s[:, g, n * P : (n + 1) * P], x_w[g, c][:].bitcast(E4M3), x_s[g, c][:],
                                    start=(g == 0), stop=(g == GROUPS - 1))
            bent = ring.tile([P, BANK], F32, name="bent", tag="size", bufs=3)
            nc.scalar.activation(bent[:], acc[:], ACT.Tanh)
            return bent

        def finish(n, c, bent):
            factor = charts[n // 2][:, n % 2, half(c)]
            nc.vector.tensor_tensor(factor, bent[:], factor, MULT)
            nc.sync.dma_start(out_0[n * P : (n + 1) * P, half(c)], factor)

        look_up(0)
        dealt0 = woven_tile("dealt0")
        round_wa(0, dealt0, 0, 1)
        quantise_wa(0, dealt0, 0, 1)
        deal_wb_words(0)
        deal_wb_scales(0)
        first_stage(0, [0])
        nc.vector.tensor_scalar(sizes[0][:, half(0)], sizes[0][:, half(0)], gain_sb[:, 0, 0:1], None, MULT)
        look_up(1)
        first_stage(0, [1])
        apply_gain(0, [1])
        round_wa(0, dealt0, 1, 2)
        round_wa(0, dealt0, 2, 4)
        quantise_wa(0, dealt0, 1, 2)
        quantise_wa(0, dealt0, 2, 4)
        deal_wb_scales(1)
        put(0, [0])
        put(0, [1])
        first_stage(1, [0, 1])
        apply_gain(1, [0, 1])
        dealt1 = woven_tile("dealt1")
        round_wa(1, dealt1, 0, PACK)
        deal_wb_words(1)
        quantise_wa(1, dealt1, 0, PACK)
        chart_rows = chart.rearrange("(j s p) m -> j p s m", s=2, p=P)
        for j in range(N // (2 * P)):
            charts.append(big([P, 2, M], F32, "chart%d" % j))
            nc.sync.dma_start(charts[j][:], chart_rows[j])

        later = {4: [("page", 0), ("page", 1)], 5: [("x", 0), ("x", 1)], 6: [("page", 2), ("page", 3)]}
        last = SLICES - 1
        for i in range(last):
            if i + 2 < SLICES:
                first_stage(i + 2, [0, 1])
            for kind, c in later.get(i, []):
                if kind == "x":
                    quantise_x(0, c, weave(nc.scalar.copy, x_pairs[0], c))
                else:
                    quantise_page(0, c, weave(nc.scalar.copy, page_pairs[0], c))
            if i > 0:
                put(i, [0, 1])
                fetch(i - 1, [0, 1])
            nc.sync.dma_start(out1_rows[i // PACK, i % PACK], pages[i][:])
            round_page(i, slice(0, T2))
            if i > 0:
                round_x(i - 1, slice(0, M))
            if i + 2 < SLICES:
                apply_gain(i + 2, [0, 1])
        store_plane_scales(0)

        fetch(last - 1, [0, 1])
        round_x(last - 1, slice(0, M))
        put(last, [0, 1])
        nc.sync.dma_start(out1_rows[last // PACK, last % PACK], pages[last][:])
        fetch(last, [0])
        fetch(last, [1])
        round_page(last, half(0))
        round_page(last, half(1))
        wp0 = weave(nc.scalar.copy, page_pairs[1], 0)
        round_x(last, half(0))
        round_x(last, half(1))
        quantise_page(1, 0, wp0)
        wx0 = weave(nc.vector.tensor_copy, x_pairs[1], 0)
        wx1 = weave(nc.vector.tensor_copy, x_pairs[1], 1)
        quantise_x(1, 0, wx0)
        quantise_x(1, 1, wx1)
        round_page(last, half(2))
        round_page(last, half(3))
        quantise_page(1, 1, weave(nc.scalar.copy, page_pairs[1], 1))
        units = [(n, c) for c in range(M // BANK) for n in range(N // P)]
        for u, (n, c) in enumerate(units):
            if u == 0:
                wp3 = weave(nc.vector.tensor_copy, page_pairs[1], 3)
            bent = score(n, c)
            finish(n, c, bent)
            if u == 0:
                quantise_page(1, 3, wp3)
            if u == 3:
                quantise_page(1, 2, weave(nc.scalar.copy, page_pairs[1], 2))
                store_plane_scales(1)
